import numpy as np
import ml_dtypes


def mxq(x, axis, fmt="e4m3"):
    dtype, down = {"e4m3": (ml_dtypes.float8_e4m3fn, 7), "e5m2": (ml_dtypes.float8_e5m2, 14)}[fmt]
    v = np.moveaxis(np.asarray(x, np.float32).astype(ml_dtypes.bfloat16).astype(np.float64), axis, -1)
    blocks = v.reshape(v.shape[:-1] + (-1, 32))
    amax = np.abs(blocks).max(-1, keepdims=True)
    byte = np.maximum(np.where(amax > 0, np.frexp(amax)[1] - 1 + 127, 0) - down, 1)
    scale = np.exp2(byte - 127.0)
    codes = (blocks / scale).astype(np.float32).astype(dtype).astype(np.float64)
    return np.moveaxis((codes * scale).reshape(v.shape), -1, axis)


WIDE = False


def mx_kscale(k):
    if not WIDE:
        return np.ones(k)
    levels = np.array([10, -10, 5, -5, 0])
    if k % 512:
        return np.exp2(np.random.permutation(np.resize(levels, k // 32))).repeat(32)
    a = np.empty((k // 512, 16))
    for p in range(k // 512):
        a[p, :8] = np.random.permutation(np.resize(levels, 8))
        for g in range(8):
            far = levels[np.abs(levels - a[p, g]) >= 10]
            a[p, g + 8] = far[np.random.randint(len(far))]
    return np.exp2(a.ravel()).repeat(32)


def f64(x):
    return np.asarray(x).astype(np.float64)


def striped(idx):
    return np.tile(idx.reshape(-1, 16).T, (8, 1)).astype(np.uint16)


def unstriped(offs):
    return offs[:16].T.reshape(-1).astype(np.int64)


E2M1 = np.array([0.0, 0.5, 1.0, 1.5, 2.0, 3.0, 4.0, 6.0, -0.0, -0.5, -1.0, -1.5, -2.0, -3.0, -4.0, -6.0])


def pack_weight(w, fmt):
    k, n = w.shape
    w = f64(np.asarray(w, np.float32).astype(ml_dtypes.bfloat16)).reshape(k // 32, 32, n)
    amax = np.abs(w).max(1)
    if fmt == "e4m3":
        byte = np.frexp(amax)[1] - 1 + 127 - 7
    else:
        mant, ex = np.frexp(amax / 6.0)
        byte = np.where(mant > 0.5, ex, ex - 1) + 127
    byte = np.clip(np.where(amax > 0, byte, 1), 1, 254)
    scaled = (w * np.exp2(127.0 - byte)[:, None, :]).reshape(k, n).astype(np.float32)
    by_word = np.ascontiguousarray(scaled.reshape(k // 512, 128, 4, n).transpose(0, 1, 3, 2))
    if fmt == "e4m3":
        words = by_word.astype(ml_dtypes.float8_e4m3fn).view(np.uint8)
    else:
        c = by_word.astype(ml_dtypes.float4_e2m1fn).view(np.uint8) & 0xF
        words = (c[..., 0::2] | (c[..., 1::2] << 4)).reshape(k // 512, 128, 2 * n)
    return np.ascontiguousarray(words), np.ascontiguousarray(byte.astype(np.uint8).reshape(k // 512, 16, n))


def unpack_weight(words, scales, fmt):
    g, _, n = scales.shape
    words = np.ascontiguousarray(words).reshape(g, 128, n, -1)
    if fmt == "e4m3":
        vals = words.view(ml_dtypes.float8_e4m3fn).astype(np.float64)
    else:
        nib = np.empty((g, 128, n, 4), np.uint8)
        nib[..., 0::2] = words & 0xF
        nib[..., 1::2] = words >> 4
        vals = E2M1[nib]
    vals = vals * np.repeat(np.exp2(scales.astype(np.float64) - 127.0), 8, axis=1)[..., None]
    return vals.transpose(0, 1, 3, 2).reshape(g * 512, n)


def gelu(v):
    return 0.5 * v * (1.0 + np.tanh(np.sqrt(2.0 / np.pi) * (v + 0.044715 * v**3)))


def bf(x):
    return np.asarray(x, np.float32).astype(ml_dtypes.bfloat16)

def planes(Y):
    n, m = Y.shape
    b = f64(bf(Y)).reshape(n // 32, 32, m)
    amax = np.abs(b).max(1)
    byte = np.clip(np.where(amax > 0, np.frexp(amax)[1] - 1 + 127 - 7, 1), 1, 254)
    codes = (b * np.exp2(127.0 - byte)[:, None, :]).reshape(n, m).astype(np.float32).astype(ml_dtypes.float8_e4m3fn).view(np.uint8)
    words = codes.reshape(n // 512, 128, 4, m).transpose(0, 1, 3, 2)
    return np.ascontiguousarray(words), np.ascontiguousarray(byte.astype(np.uint8).reshape(n // 512, 16, m))


K, H, N, T, T2, S = 512, 1024, 512, 4096, 2048, 1024


def setup_inputs():
    n = np.random.standard_normal
    s = mx_kscale(K)[:, None]
    u = mx_kscale(H)[:, None]
    tab_words, tab_scales = pack_weight(n((K, T)) * s, "e4m3")
    tab2_words, tab2_scales = pack_weight(n((K, T2)) * s, "e4m3")
    wf_words, wf_scales = pack_weight(0.6 * n((K, H)) / np.sqrt(K) / s, "e2m1")
    wr = (0.6 * n((K, H)) / np.sqrt(K) / s).astype(np.float32)
    kf = (np.exp(0.3 * n(H)) * u[:, 0]).astype(np.float32)
    kr = (np.exp(0.3 * n(H)) * u[:, 0]).astype(np.float32)
    ws = n((H, N)) / np.sqrt(H) * np.exp(0.8 * n(N))[None, :] / u
    ws_words, ws_scales = pack_weight(ws, "e4m3")
    offs = striped(np.random.permutation(T)[:S])
    offs2 = striped(np.random.permutation(T2)[:S])
    return {"tab_words": tab_words, "tab_scales": tab_scales,
            "tab2_words": tab2_words, "tab2_scales": tab2_scales,
            "offs": offs, "offs2": offs2,
            "wf_words": wf_words, "wf_scales": wf_scales, "wr": wr,
            "kf": kf, "kr": kr, "ws_words": ws_words, "ws_scales": ws_scales}


def reference(tab_words, tab_scales, tab2_words, tab2_scales, offs, offs2,
              wf_words, wf_scales, wr, kf, kr, ws_words, ws_scales):
    v = unpack_weight(tab_words, tab_scales, "e4m3")[:, unstriped(offs)]
    v2 = unpack_weight(tab2_words, tab2_scales, "e4m3")[:, unstriped(offs2)]
    wf = unpack_weight(wf_words, wf_scales, "e2m1")
    ws = unpack_weight(ws_words, ws_scales, "e4m3")
    a = wf.T @ v
    b = mxq(f64(wr), 0, "e4m3").T @ v2
    h = f64(kf)[:, None] * np.exp(a) - f64(kr)[:, None] * np.exp(b)
    y = ws.T @ mxq(h, 0, "e4m3")
    words, scales = planes(y)
    return y, words, scales

@@ -1,0 +1,263 @@
+from contextlib import ExitStack
+
+import concourse.mybir as mybir
+
+K, H, N, T, T2, S = 512, 1024, 512, 4096, 2048, 1024
+FLOPS = 2 * K * H * S * 2 + 2 * H * N * S
+
+F32 = mybir.dt.float32
+BF16 = mybir.dt.bfloat16
+I32 = mybir.dt.int32
+U32 = mybir.dt.uint32
+U16 = mybir.dt.uint16
+U8 = mybir.dt.uint8
+FP8X4 = mybir.dt.float8_e4m3fn_x4
+FP4X4 = mybir.dt.float4_e2m1fn_x4
+EXP = mybir.ActivationFunctionType.Exp
+COPY = mybir.ActivationFunctionType.Copy
+MULT = mybir.AluOpType.mult
+SUB = mybir.AluOpType.subtract
+
+P = 128
+PACK = 4
+PASS = P * PACK
+GROUPS = H // PASS
+HALF = 512
+LIST_COLS = HALF // 16
+WS_ROW = 8
+
+
+def tile_list_reaction_rates_kernel(tc, tab_words, tab_scales, tab2_words, tab2_scales, offs, offs2,
+                                             wf_words, wf_scales, wr, kf, kr, ws_words, ws_scales,
+                                             out_0, out_1, out_2):
+    nc = tc.nc
+    with ExitStack() as ctx:
+        lists = ctx.enter_context(tc.tile_pool(name="lists", bufs=1))
+        keep = ctx.enter_context(tc.tile_pool(name="keep", bufs=1))
+        psum = ctx.enter_context(tc.psum_pool(name="psum", bufs=1))
+
+        def tile(shape, dtype, name, tag=None):
+            return keep.tile(shape, dtype, name=name, tag=tag or name, align_bytes=64)
+
+        def load_plane(memset_engine, dma_engine, plane, row, rows, src):
+            memset_engine.memset(plane[:].bitcast(I32), 0)
+            for q in range(4):
+                dma_engine.dma_start(out=plane[32 * q + row : 32 * q + row + rows, :].bitcast(I32), in_=src(q).bitcast(I32))
+
+        idx2 = lists.tile([P, S // 16], U16, name="idx2")
+        nc.sync.dma_start(idx2[:], offs2)
+        tab2_plane = tile([P, T2], U8, "tab2_plane")
+        for q in range(4):
+            nc.sync.dma_start(out=tab2_plane[32 * q : 32 * q + 32, :].bitcast(I32),
+                              in_=tab2_scales[0, 4 * q : 4 * q + 4, :].bitcast(I32).unsqueeze(0).broadcast_to([8, 4, T2 // 4]))
+        idx = lists.tile([P, S // 16], U16, name="idx")
+        nc.sync.dma_start(idx[:], offs)
+        tab2_w = tile([P, T2], I32, "tab2_w")
+        nc.sync.dma_start(out=tab2_w[:], in_=tab2_words[0].rearrange("p n t -> p (n t)").bitcast(I32))
+        tab_plane = tile([P, T], U8, "tab_plane")
+        load_plane(nc.vector, nc.sync, tab_plane, 0, 4, lambda q: tab_scales[0, 4 * q : 4 * q + 4, :])
+        warm = tile([P, 2], F32, "warm")
+        nc.vector.memset(warm[:, 0:1], 0.0)
+        nc.scalar.activation(warm[:, 1:2], warm[:, 0:1], EXP)
+
+        def load_wr(g):
+            raw = tile([P, PACK, PASS], F32, "wr_raw%d" % g)
+            nc.sync.dma_start(out=raw[:], in_=wr[:, g * PASS : (g + 1) * PASS].rearrange("(p j) c -> p j c", j=PACK))
+            return raw
+
+        wr_raw0 = load_wr(0)
+        wf_plane = tile([P, H], U8, "wf_plane")
+        load_plane(nc.gpsimd, nc.sync, wf_plane, 0, 4, lambda q: wf_scales[0, 4 * q : 4 * q + 4, :])
+        wf_raw = tile([P, 2 * H], U8, "wf_raw")
+        nc.sync.dma_start(out=wf_raw[:].bitcast(I32), in_=wf_words[0].bitcast(I32))
+        tab_w = tile([P, T], I32, "tab_w")
+        nc.sync.dma_start(out=tab_w[:], in_=tab_words[0].rearrange("p n t -> p (n t)").bitcast(I32))
+        wr_raw1 = load_wr(1)
+        ws_raw = tile([P, GROUPS * N], I32, "ws_raw")
+        nc.sync.dma_start(
+            out=ws_raw[:].rearrange("p (a n) -> p a n", a=GROUPS),
+            in_=ws_words.rearrange("a p n t -> p a (n t)").bitcast(I32),
+        )
+        ws_plane = tile([P, N], U8, "ws_plane")
+        load_plane(nc.gpsimd, nc.sync, ws_plane, WS_ROW, 8, lambda q: ws_scales[:, 4 * q : 4 * q + 4, :])
+
+        kr_t = tile([P, GROUPS, PACK], F32, "kr_t")
+        nc.gpsimd.dma_start(out=kr_t[:], in_=kr.rearrange("(g p t) -> p g t", p=P, t=PACK))
+        kf_t = tile([P, GROUPS, PACK], F32, "kf_t")
+        nc.gpsimd.dma_start(out=kf_t[:], in_=kf.rearrange("(g p t) -> p g t", p=P, t=PACK))
+
+        def gather(window, offsets, half, dtype, name):
+            got = tile([P, HALF], dtype, "%s%d" % (name, half))
+            nc.vector.tensor_copy(got[:], window.indirect(offsets[:, half * LIST_COLS : (half + 1) * LIST_COLS]))
+            return got
+
+        def quantize(grouped, codes, plane):
+            nc.vector.quantize_mx(out=codes.bitcast(FP8X4), scales=plane, in_=grouped)
+
+        def cast_wr(g, raw, u):
+            grouped = tile([P, 2 * PASS], BF16, "wr_bf%d%d" % (g, u))
+            nc.scalar.copy(
+                out=grouped[:].rearrange("p (t m j) -> p m j t", t=2, j=PACK),
+                in_=raw[:].rearrange("p j (m u t) -> p u m j t", u=2, t=2)[:, u],
+            )
+            codes = tile([P, 2 * P], U32, "wr_q%d%d" % (g, u))
+            plane = tile([P, 2 * P], U8, "wr_s%d%d" % (g, u))
+            quantize(grouped[:], codes[:], plane[:])
+            return codes, plane
+
+        v2_s, v2_w, v_s, v_w = {}, {}, {}, {}
+        wr_q = {}
+        v2_s[0] = gather(tab2_plane[:], idx2, 0, U8, "v2_s")
+        v2_w[0] = gather(tab2_w[:].bitcast(U32), idx2, 0, U32, "v2_w")
+        wr_q[0, 0] = cast_wr(0, wr_raw0, 0)
+        wr_q[0, 1] = cast_wr(0, wr_raw0, 1)
+        v2_s[1] = gather(tab2_plane[:], idx2, 1, U8, "v2_s")
+        v2_w[1] = gather(tab2_w[:].bitcast(U32), idx2, 1, U32, "v2_w")
+
+        def exp_block(name, g, half, stationary, moving, factor, on_scalar):
+            e = tile([P, PACK, HALF], F32, "%s%d%d" % (name, g, half))
+            for t in range(PACK):
+                acc = psum.tile([P, HALF], F32, name="first", tag="first", bufs=4)
+                w, w_scale = stationary(t)
+                nc.tensor.matmul_mx(out=acc[:], lhsT=w, lhsT_scale=w_scale, rhs=moving[0], rhs_scale=moving[1],
+                                    start=True, stop=True)
+                nc.scalar.activation(e[:, t, :], acc[:], EXP)
+            for t in range(PACK):
+                if t in on_scalar:
+                    nc.scalar.activation(e[:, t, :], e[:, t, :], COPY, scale=factor[:, g, t : t + 1])
+                else:
+                    nc.vector.tensor_scalar(e[:, t, :], e[:, t, :], factor[:, g, t : t + 1], None, MULT)
+            return e
+
+        def reverse(g, half, on_scalar=()):
+            def stationary(t):
+                codes, plane = wr_q[g, t // 2]
+                cols = slice((t % 2) * P, (t % 2 + 1) * P)
+                return codes[:, cols].bitcast(FP8X4), plane[:, cols]
+            moving = (v2_w[half][:].bitcast(FP8X4), v2_s[half][:])
+            return exp_block("eb", g, half, stationary, moving, kr_t, on_scalar)
+
+        wf_q = {}
+
+        def deal_wf(g):
+            words = tile([P, 2 * PASS], U8, "wf_w%d" % g)
+            nc.vector.tensor_copy(
+                out=words[:].bitcast(U16).rearrange("p (t m) -> p t m", t=PACK),
+                in_=wf_raw[:, 2 * g * PASS : 2 * (g + 1) * PASS].bitcast(U16).rearrange("p (m t) -> p t m", t=PACK),
+            )
+            plane = tile([P, PASS], U8, "wf_s%d" % g)
+            nc.vector.tensor_copy(
+                out=plane[:].rearrange("p (t m) -> p t m", t=PACK),
+                in_=wf_plane[:, g * PASS : (g + 1) * PASS].rearrange("p (m t) -> p t m", t=PACK),
+            )
+            wf_q[g] = words, plane
+
+        def forward(g, half, on_scalar=()):
+            def stationary(t):
+                words, plane = wf_q[g]
+                return words[:, 2 * t * P : 2 * (t + 1) * P].bitcast(FP4X4), plane[:, t * P : (t + 1) * P]
+            moving = (v_w[half][:].bitcast(FP8X4), v_s[half][:])
+            return exp_block("ea", g, half, stationary, moving, kf_t, on_scalar)
+
+        h_q = {}
+
+        def net_rate(g, ea, eb, half, c0, width):
+            grouped = tile([P, PACK * width], BF16, "h_bf%d_%d" % (g, half * HALF + c0))
+            cols = slice(c0, c0 + width)
+            nc.vector.tensor_tensor(
+                grouped[:].rearrange("p (c i t) -> p c t i", i=2, t=PACK),
+                ea[:, :, cols].rearrange("p t (c i) -> p c t i", i=2),
+                eb[:, :, cols].rearrange("p t (c i) -> p c t i", i=2),
+                SUB,
+            )
+            codes = tile([P, width], U32, "h_q%d_%d" % (g, half * HALF + c0))
+            plane = tile([P, width], U8, "h_s%d_%d" % (g, half * HALF + c0))
+            quantize(grouped[:], codes[:], plane[:])
+            h_q[g, half, c0] = codes, plane, width
+
+        def h_operand(g, half, c0, width):
+            for (gg, hh, start), (codes, plane, wide) in h_q.items():
+                if gg == g and hh == half and start <= c0 < start + wide:
+                    cols = slice(c0 - start, c0 - start + width)
+                    return codes[:, cols].bitcast(FP8X4), plane[:, cols]
+
+        ws_w = tile([P, GROUPS * N], U32, "ws_w")
+        ws_s = tile([P, N], U8, "ws_s")
+
+        def deal_ws():
+            for a in range(GROUPS):
+                nc.vector.tensor_copy(
+                    out=ws_w[:, a * N : (a + 1) * N].rearrange("p (u t m) -> p u m t", u=2, t=2),
+                    in_=ws_raw[:, a * N : (a + 1) * N].bitcast(U32).rearrange("p (m u t) -> p u m t", u=2, t=2),
+                )
+            nc.vector.tensor_copy(
+                out=ws_s[:].rearrange("p (t m) -> p t m", t=PACK),
+                in_=ws_plane[:].rearrange("p (m t) -> p t m", t=PACK),
+            )
+
+        y_plane = tile([P, S], U8, "y_plane")
+        y_rows = out_0.rearrange("(p t) n -> p t n", t=PACK)
+        y_words = out_1[0].rearrange("p n t -> p (n t)").bitcast(I32)
+
+        def production(half, c0, width):
+            first = half * HALF + c0
+            y = tile([P, PACK, width], F32, "y%d" % first)
+            per_bank = HALF // width
+            for b in range(PACK // per_bank):
+                acc = psum.tile([P, per_bank, width], F32, name="second", tag="second", bufs=4)
+                for s in range(per_bank):
+                    t = b * per_bank + s
+                    for g in range(GROUPS):
+                        codes, plane = h_operand(g, half, c0, width)
+                        nc.tensor.matmul_mx(
+                            out=acc[:, s, :],
+                            lhsT=ws_w[:, g * N + t * P : g * N + (t + 1) * P].bitcast(FP8X4),
+                            lhsT_scale=ws_s[WS_ROW + 4 * g : P, t * P : (t + 1) * P],
+                            rhs=codes, rhs_scale=plane, start=(g == 0), stop=(g == GROUPS - 1))
+                rows = slice(b * per_bank, (b + 1) * per_bank)
+                nc.scalar.copy(out=y[:, rows, :], in_=acc[:])
+            nc.sync.dma_start(out=y_rows[:, :, first : first + width], in_=y[:])
+            return y
+
+        def planes(y, half, c0, width):
+            first = half * HALF + c0
+            grouped = tile([P, PACK * width], BF16, "y_bf%d" % first)
+            nc.vector.tensor_copy(
+                out=grouped[:].rearrange("p (c i t) -> p c t i", i=2, t=PACK),
+                in_=y[:].rearrange("p t (c i) -> p c t i", i=2),
+            )
+            codes = tile([P, width], U32, "y_q%d" % first)
+            quantize(grouped[:], codes[:], y_plane[:, first : first + width])
+            nc.sync.dma_start(out=y_words[:, first : first + width], in_=codes[:].bitcast(I32))
+
+        eb00 = reverse(0, 0)
+        v_s[0] = gather(tab_plane[:], idx, 0, U8, "v_s")
+        deal_wf(0)
+        v_w[0] = gather(tab_w[:].bitcast(U32), idx, 0, U32, "v_w")
+        ea00 = forward(0, 0)
+        eb01 = reverse(0, 1)
+        net_rate(0, ea00, eb00, 0, 0, HALF)
+        deal_wf(1)
+        wr_q[1, 0] = cast_wr(1, wr_raw1, 0)
+        wr_q[1, 1] = cast_wr(1, wr_raw1, 1)
+        ea10 = forward(1, 0)
+        eb10 = reverse(1, 0)
+        v_s[1] = gather(tab_plane[:], idx, 1, U8, "v_s")
+        v_w[1] = gather(tab_w[:].bitcast(U32), idx, 1, U32, "v_w")
+        deal_ws()
+        net_rate(1, ea10, eb10, 0, 0, HALF)
+        ea01 = forward(0, 1)
+        y0 = production(0, 0, HALF)
+        net_rate(0, ea01, eb01, 1, 0, HALF)
+        planes(y0, 0, 0, HALF)
+        eb11 = reverse(1, 1)
+        ea11 = forward(1, 1, on_scalar=(0, 1, 2, 3))
+        net_rate(1, ea11, eb11, 1, 0, 256)
+        y1 = production(1, 0, 256)
+        net_rate(1, ea11, eb11, 1, 256, 256)
+        y2 = production(1, 256, 256)
+        planes(y1, 1, 0, 256)
+        planes(y2, 1, 256, 256)
+        for q in range(4):
+            (nc.scalar if q % 2 else nc.sync).dma_start(
+                out=out_2[0, 4 * q : 4 * q + 4, :].bitcast(I32), in_=y_plane[32 * q : 32 * q + 4, :].bitcast(I32))

@@ -23,7 +23,6 @@ PACK = 4
 PASS = P * PACK
 GROUPS = H // PASS
 HALF = 512
-LIST_COLS = HALF // 16
 WS_ROW = 8
 
 
@@ -86,121 +85,68 @@ def tile_list_reaction_rates_kernel(tc, tab_words, tab_scales, tab2_words, tab2_
         kf_t = tile([P, GROUPS, PACK], F32, "kf_t")
         nc.gpsimd.dma_start(out=kf_t[:], in_=kf.rearrange("(g p t) -> p g t", p=P, t=PACK))
 
-        def gather(window, offsets, half, dtype, name):
-            got = tile([P, HALF], dtype, "%s%d" % (name, half))
-            nc.vector.tensor_copy(got[:], window.indirect(offsets[:, half * LIST_COLS : (half + 1) * LIST_COLS]))
+        def gather(window, offsets, first, count, dtype, name):
+            got = tile([P, count], dtype, "%s%d" % (name, first))
+            nc.vector.tensor_copy(got[:], window.indirect(offsets[:, first // 16 : (first + count) // 16]))
             return got
 
         def quantize(grouped, codes, plane):
             nc.vector.quantize_mx(out=codes.bitcast(FP8X4), scales=plane, in_=grouped)
 
-        def cast_wr(g, raw, u):
-            grouped = tile([P, 2 * PASS], BF16, "wr_bf%d%d" % (g, u))
+        def cast_wr(raw, grouped, u):
             nc.scalar.copy(
-                out=grouped[:].rearrange("p (t m j) -> p m j t", t=2, j=PACK),
+                out=grouped[:, 2 * u * PASS : 2 * (u + 1) * PASS].rearrange("p (t m j) -> p m j t", t=2, j=PACK),
                 in_=raw[:].rearrange("p j (m u t) -> p u m j t", u=2, t=2)[:, u],
             )
-            codes = tile([P, 2 * P], U32, "wr_q%d%d" % (g, u))
-            plane = tile([P, 2 * P], U8, "wr_s%d%d" % (g, u))
-            quantize(grouped[:], codes[:], plane[:])
-            return codes, plane
 
-        v2_s, v2_w, v_s, v_w = {}, {}, {}, {}
-        wr_q = {}
-        v2_s[0] = gather(tab2_plane[:], idx2, 0, U8, "v2_s")
-        v2_w[0] = gather(tab2_w[:].bitcast(U32), idx2, 0, U32, "v2_w")
-        wr_q[0, 0] = cast_wr(0, wr_raw0, 0)
-        wr_q[0, 1] = cast_wr(0, wr_raw0, 1)
-        v2_s[1] = gather(tab2_plane[:], idx2, 1, U8, "v2_s")
-        v2_w[1] = gather(tab2_w[:].bitcast(U32), idx2, 1, U32, "v2_w")
+        wr_w = [tile([P, PASS], U32, "wr_w%d" % g) for g in range(GROUPS)]
+        wr_s = [tile([P, PASS], U8, "wr_s%d" % g) for g in range(GROUPS)]
+        ea = [tile([P, PACK, S], F32, "ea%d" % g) for g in range(GROUPS)]
+        eb = [tile([P, PACK, S], F32, "eb%d" % g) for g in range(GROUPS)]
+        h_w = [tile([P, S], U32, "h_w%d" % g) for g in range(GROUPS)]
+        h_s = [tile([P, S], U8, "h_s%d" % g) for g in range(GROUPS)]
+        v_w, v2_w = {}, {}
 
-        def exp_block(name, g, half, stationary, moving, factor, on_scalar):
-            e = tile([P, PACK, HALF], F32, "%s%d%d" % (name, g, half))
+        def exponential(e, t, half, w, w_scale, cells, cells_scale):
+            acc = psum.tile([P, HALF], F32, name="first", tag="first", bufs=4)
+            cols = slice(half * HALF, (half + 1) * HALF)
+            nc.tensor.matmul_mx(out=acc[:], lhsT=w, lhsT_scale=w_scale, rhs=cells[half][:].bitcast(FP8X4),
+                                rhs_scale=cells_scale[:, cols], start=True, stop=True)
+            nc.scalar.activation(e[:, t, cols], acc[:], EXP)
+
+        def reverse(g, t, half):
+            cols = slice(t * P, (t + 1) * P)
+            exponential(eb[g], t, half, wr_w[g][:, cols].bitcast(FP8X4), wr_s[g][:, cols], v2_w, v2_s)
+
+        def forward(g, t, half):
+            first = g * PASS + t * P
+            exponential(ea[g], t, half, wf_w[:, 2 * first : 2 * (first + P)].bitcast(FP4X4), wf_s[:, first : first + P], v_w, v_s)
+
+        def scale_reverse(g, t, first, width, on_scalar):
+            e = eb[g][:, t, first : first + width]
+            if on_scalar:
+                nc.scalar.activation(e, e, COPY, scale=kr_t[:, g, t : t + 1])
+            else:
+                nc.vector.tensor_scalar(e, e, kr_t[:, g, t : t + 1], None, MULT)
+
+        def net_rate(g, first, width):
+            cols = slice(first, first + width)
+            h = tile([P, PACK, width], BF16, "h%d_%d" % (g, first))
             for t in range(PACK):
-                acc = psum.tile([P, HALF], F32, name="first", tag="first", bufs=4)
-                w, w_scale = stationary(t)
-                nc.tensor.matmul_mx(out=acc[:], lhsT=w, lhsT_scale=w_scale, rhs=moving[0], rhs_scale=moving[1],
-                                    start=True, stop=True)
-                nc.scalar.activation(e[:, t, :], acc[:], EXP)
-            for t in range(PACK):
-                if t in on_scalar:
-                    nc.scalar.activation(e[:, t, :], e[:, t, :], COPY, scale=factor[:, g, t : t + 1])
-                else:
-                    nc.vector.tensor_scalar(e[:, t, :], e[:, t, :], factor[:, g, t : t + 1], None, MULT)
-            return e
-
-        def reverse(g, half, on_scalar=()):
-            def stationary(t):
-                codes, plane = wr_q[g, t // 2]
-                cols = slice((t % 2) * P, (t % 2 + 1) * P)
-                return codes[:, cols].bitcast(FP8X4), plane[:, cols]
-            moving = (v2_w[half][:].bitcast(FP8X4), v2_s[half][:])
-            return exp_block("eb", g, half, stationary, moving, kr_t, on_scalar)
-
-        wf_q = {}
-
-        def deal_wf(g):
-            words = tile([P, 2 * PASS], U8, "wf_w%d" % g)
+                nc.vector.scalar_tensor_tensor(h[:, t, :], ea[g][:, t, cols], kf_t[:, g, t : t + 1], eb[g][:, t, cols], MULT, SUB)
+            grouped = tile([P, PACK * width], BF16, "h_bf%d_%d" % (g, first))
             nc.vector.tensor_copy(
-                out=words[:].bitcast(U16).rearrange("p (t m) -> p t m", t=PACK),
-                in_=wf_raw[:, 2 * g * PASS : 2 * (g + 1) * PASS].bitcast(U16).rearrange("p (m t) -> p t m", t=PACK),
+                out=grouped[:].rearrange("p (c i t) -> p c t i", i=4, t=PACK),
+                in_=h[:].rearrange("p t (c i) -> p c t i", i=4),
             )
-            plane = tile([P, PASS], U8, "wf_s%d" % g)
-            nc.vector.tensor_copy(
-                out=plane[:].rearrange("p (t m) -> p t m", t=PACK),
-                in_=wf_plane[:, g * PASS : (g + 1) * PASS].rearrange("p (m t) -> p t m", t=PACK),
-            )
-            wf_q[g] = words, plane
-
-        def forward(g, half, on_scalar=()):
-            def stationary(t):
-                words, plane = wf_q[g]
-                return words[:, 2 * t * P : 2 * (t + 1) * P].bitcast(FP4X4), plane[:, t * P : (t + 1) * P]
-            moving = (v_w[half][:].bitcast(FP8X4), v_s[half][:])
-            return exp_block("ea", g, half, stationary, moving, kf_t, on_scalar)
-
-        h_q = {}
-
-        def net_rate(g, ea, eb, half, c0, width):
-            grouped = tile([P, PACK * width], BF16, "h_bf%d_%d" % (g, half * HALF + c0))
-            cols = slice(c0, c0 + width)
-            nc.vector.tensor_tensor(
-                grouped[:].rearrange("p (c i t) -> p c t i", i=2, t=PACK),
-                ea[:, :, cols].rearrange("p t (c i) -> p c t i", i=2),
-                eb[:, :, cols].rearrange("p t (c i) -> p c t i", i=2),
-                SUB,
-            )
-            codes = tile([P, width], U32, "h_q%d_%d" % (g, half * HALF + c0))
-            plane = tile([P, width], U8, "h_s%d_%d" % (g, half * HALF + c0))
-            quantize(grouped[:], codes[:], plane[:])
-            h_q[g, half, c0] = codes, plane, width
-
-        def h_operand(g, half, c0, width):
-            for (gg, hh, start), (codes, plane, wide) in h_q.items():
-                if gg == g and hh == half and start <= c0 < start + wide:
-                    cols = slice(c0 - start, c0 - start + width)
-                    return codes[:, cols].bitcast(FP8X4), plane[:, cols]
-
-        ws_w = tile([P, GROUPS * N], U32, "ws_w")
-        ws_s = tile([P, N], U8, "ws_s")
-
-        def deal_ws():
-            for a in range(GROUPS):
-                nc.vector.tensor_copy(
-                    out=ws_w[:, a * N : (a + 1) * N].rearrange("p (u t m) -> p u m t", u=2, t=2),
-                    in_=ws_raw[:, a * N : (a + 1) * N].bitcast(U32).rearrange("p (m u t) -> p u m t", u=2, t=2),
-                )
-            nc.vector.tensor_copy(
-                out=ws_s[:].rearrange("p (t m) -> p t m", t=PACK),
-                in_=ws_plane[:].rearrange("p (m t) -> p t m", t=PACK),
-            )
+            quantize(grouped[:], h_w[g][:, cols], h_s[g][:, cols])
 
         y_plane = tile([P, S], U8, "y_plane")
         y_rows = out_0.rearrange("(p t) n -> p t n", t=PACK)
         y_words = out_1[0].rearrange("p n t -> p (n t)").bitcast(I32)
 
-        def production(half, c0, width):
-            first = half * HALF + c0
+        def production(first, width):
+            cols = slice(first, first + width)
             y = tile([P, PACK, width], F32, "y%d" % first)
             per_bank = HALF // width
             for b in range(PACK // per_bank):
@@ -208,56 +154,89 @@ def tile_list_reaction_rates_kernel(tc, tab_words, tab_scales, tab2_words, tab2_
                 for s in range(per_bank):
                     t = b * per_bank + s
                     for g in range(GROUPS):
-                        codes, plane = h_operand(g, half, c0, width)
                         nc.tensor.matmul_mx(
                             out=acc[:, s, :],
                             lhsT=ws_w[:, g * N + t * P : g * N + (t + 1) * P].bitcast(FP8X4),
                             lhsT_scale=ws_s[WS_ROW + 4 * g : P, t * P : (t + 1) * P],
-                            rhs=codes, rhs_scale=plane, start=(g == 0), stop=(g == GROUPS - 1))
+                            rhs=h_w[g][:, cols].bitcast(FP8X4), rhs_scale=h_s[g][:, cols], start=(g == 0), stop=(g == GROUPS - 1))
                 rows = slice(b * per_bank, (b + 1) * per_bank)
                 nc.scalar.copy(out=y[:, rows, :], in_=acc[:])
             nc.sync.dma_start(out=y_rows[:, :, first : first + width], in_=y[:])
             return y
 
-        def planes(y, half, c0, width):
-            first = half * HALF + c0
+        def planes(y, first, width, copy):
             grouped = tile([P, PACK * width], BF16, "y_bf%d" % first)
-            nc.vector.tensor_copy(
-                out=grouped[:].rearrange("p (c i t) -> p c t i", i=2, t=PACK),
-                in_=y[:].rearrange("p t (c i) -> p c t i", i=2),
+            copy(
+                out=grouped[:].rearrange("p (c i t) -> p c t i", i=4, t=PACK),
+                in_=y[:].rearrange("p t (c i) -> p c t i", i=4),
             )
             codes = tile([P, width], U32, "y_q%d" % first)
             quantize(grouped[:], codes[:], y_plane[:, first : first + width])
             nc.sync.dma_start(out=y_words[:, first : first + width], in_=codes[:].bitcast(I32))
 
-        eb00 = reverse(0, 0)
-        v_s[0] = gather(tab_plane[:], idx, 0, U8, "v_s")
-        deal_wf(0)
-        v_w[0] = gather(tab_w[:].bitcast(U32), idx, 0, U32, "v_w")
-        ea00 = forward(0, 0)
-        eb01 = reverse(0, 1)
-        net_rate(0, ea00, eb00, 0, 0, HALF)
-        deal_wf(1)
-        wr_q[1, 0] = cast_wr(1, wr_raw1, 0)
-        wr_q[1, 1] = cast_wr(1, wr_raw1, 1)
-        ea10 = forward(1, 0)
-        eb10 = reverse(1, 0)
-        v_s[1] = gather(tab_plane[:], idx, 1, U8, "v_s")
-        v_w[1] = gather(tab_w[:].bitcast(U32), idx, 1, U32, "v_w")
-        deal_ws()
-        net_rate(1, ea10, eb10, 0, 0, HALF)
-        ea01 = forward(0, 1)
-        y0 = production(0, 0, HALF)
-        net_rate(0, ea01, eb01, 1, 0, HALF)
-        planes(y0, 0, 0, HALF)
-        eb11 = reverse(1, 1)
-        ea11 = forward(1, 1, on_scalar=(0, 1, 2, 3))
-        net_rate(1, ea11, eb11, 1, 0, 256)
-        y1 = production(1, 0, 256)
-        net_rate(1, ea11, eb11, 1, 256, 256)
-        y2 = production(1, 256, 256)
-        planes(y1, 1, 0, 256)
-        planes(y2, 1, 256, 256)
+        v2_s = gather(tab2_plane[:], idx2, 0, S, U8, "v2_s")
+        v2_w[0] = gather(tab2_w[:].bitcast(U32), idx2, 0, HALF, U32, "v2_w")
+        v2_w[1] = gather(tab2_w[:].bitcast(U32), idx2, HALF, HALF, U32, "v2_w")
+        wr_bf0 = tile([P, PACK * PASS], BF16, "wr_bf0")
+        for u in range(2):
+            cast_wr(wr_raw0, wr_bf0, u)
+            cols = slice(2 * u * P, 2 * (u + 1) * P)
+            quantize(wr_bf0[:, 2 * u * PASS : 2 * (u + 1) * PASS], wr_w[0][:, cols], wr_s[0][:, cols])
+        v_s = gather(tab_plane[:], idx, 0, S, U8, "v_s")
+        for t in range(PACK):
+            reverse(0, t, 0)
+            reverse(0, t, 1)
+        wf_w = tile([P, 2 * H], U8, "wf_w")
+        nc.vector.tensor_copy(
+            out=wf_w[:].bitcast(U16).rearrange("p (g t m) -> p g t m", g=GROUPS, t=PACK),
+            in_=wf_raw[:].bitcast(U16).rearrange("p (g m t) -> p g t m", g=GROUPS, t=PACK),
+        )
+        wf_s = tile([P, H], U8, "wf_s")
+        nc.vector.tensor_copy(
+            out=wf_s[:].rearrange("p (g t m) -> p g t m", g=GROUPS, t=PACK),
+            in_=wf_plane[:].rearrange("p (g m t) -> p g t m", g=GROUPS, t=PACK),
+        )
+        v_w[0] = gather(tab_w[:].bitcast(U32), idx, 0, HALF, U32, "v_w")
+        v_w[1] = gather(tab_w[:].bitcast(U32), idx, HALF, HALF, U32, "v_w")
+        for t in range(PACK):
+            scale_reverse(0, t, 0, S, on_scalar=t >= 2)
+        for t in range(PACK):
+            forward(0, t, 0)
+            forward(0, t, 1)
+        wr_bf1 = tile([P, PACK * PASS], BF16, "wr_bf1", tag="tab_w")
+        for u in range(2):
+            cast_wr(wr_raw1, wr_bf1, u)
+        quantize(wr_bf1[:], wr_w[1][:], wr_s[1][:])
+        net_rate(0, 0, S)
+        for t in range(PACK):
+            reverse(1, t, 0)
+            scale_reverse(1, t, 0, HALF, on_scalar=False)
+        for t in range(PACK):
+            forward(1, t, 0)
+        ws_w = tile([P, GROUPS * N], U32, "ws_w", tag="wr_raw1")
+        nc.vector.tensor_copy(
+            out=ws_w[:].rearrange("p (a u t m) -> p a u m t", a=GROUPS, u=2, t=2),
+            in_=ws_raw[:].bitcast(U32).rearrange("p (a m u t) -> p a u m t", a=GROUPS, u=2, t=2),
+        )
+        ws_s = tile([P, N], U8, "ws_s", tag="tab_w")
+        nc.vector.tensor_copy(
+            out=ws_s[:].rearrange("p (t m) -> p t m", t=PACK),
+            in_=ws_plane[:].rearrange("p (m t) -> p t m", t=PACK),
+        )
+        net_rate(1, 0, HALF)
+        for t in range(PACK):
+            reverse(1, t, 1)
+            scale_reverse(1, t, HALF, HALF, on_scalar=False)
+        for t in range(PACK):
+            forward(1, t, 1)
+        y0 = production(0, HALF)
+        net_rate(1, HALF, 256)
+        y1 = production(HALF, 256)
+        net_rate(1, HALF + 256, 256)
+        y2 = production(HALF + 256, 256)
+        planes(y0, 0, HALF, nc.scalar.copy)
+        planes(y1, HALF, 256, nc.vector.tensor_copy)
+        planes(y2, HALF + 256, 256, nc.vector.tensor_copy)
         for q in range(4):
             (nc.scalar if q % 2 else nc.sync).dma_start(
                 out=out_2[0, 4 * q : 4 * q + 4, :].bitcast(I32), in_=y_plane[32 * q : 32 * q + 4, :].bitcast(I32))

@@ -23,6 +23,7 @@ PACK = 4
 PASS = P * PACK
 GROUPS = H // PASS
 HALF = 512
+QUARTER = 256
 WS_ROW = 8
 
 
@@ -38,11 +39,14 @@ def tile_list_reaction_rates_kernel(tc, tab_words, tab_scales, tab2_words, tab2_
         def tile(shape, dtype, name, tag=None):
             return keep.tile(shape, dtype, name=name, tag=tag or name, align_bytes=64)
 
-        def load_plane(memset_engine, dma_engine, plane, row, rows, src):
+        def load_plane(memset_engine, plane, scales):
             memset_engine.memset(plane[:].bitcast(I32), 0)
-            for q in range(4):
-                dma_engine.dma_start(out=plane[32 * q + row : 32 * q + row + rows, :].bitcast(I32), in_=src(q).bitcast(I32))
+            for r in range(4):
+                nc.sync.dma_start(out=plane[r:P:32, :].bitcast(I32), in_=scales[0, r:16:4, :].bitcast(I32))
 
+        warm = tile([P, 2], F32, "warm")
+        nc.vector.memset(warm[:, 0:1], 0.0)
+        nc.scalar.activation(warm[:, 1:2], warm[:, 0:1], EXP)
         idx2 = lists.tile([P, S // 16], U16, name="idx2")
         nc.sync.dma_start(idx2[:], offs2)
         tab2_plane = tile([P, T2], U8, "tab2_plane")
@@ -54,10 +58,7 @@ def tile_list_reaction_rates_kernel(tc, tab_words, tab_scales, tab2_words, tab2_
         tab2_w = tile([P, T2], I32, "tab2_w")
         nc.sync.dma_start(out=tab2_w[:], in_=tab2_words[0].rearrange("p n t -> p (n t)").bitcast(I32))
         tab_plane = tile([P, T], U8, "tab_plane")
-        load_plane(nc.vector, nc.sync, tab_plane, 0, 4, lambda q: tab_scales[0, 4 * q : 4 * q + 4, :])
-        warm = tile([P, 2], F32, "warm")
-        nc.vector.memset(warm[:, 0:1], 0.0)
-        nc.scalar.activation(warm[:, 1:2], warm[:, 0:1], EXP)
+        load_plane(nc.vector, tab_plane, tab_scales)
 
         def load_wr(g):
             raw = tile([P, PACK, PASS], F32, "wr_raw%d" % g)
@@ -66,7 +67,7 @@ def tile_list_reaction_rates_kernel(tc, tab_words, tab_scales, tab2_words, tab2_
 
         wr_raw0 = load_wr(0)
         wf_plane = tile([P, H], U8, "wf_plane")
-        load_plane(nc.gpsimd, nc.sync, wf_plane, 0, 4, lambda q: wf_scales[0, 4 * q : 4 * q + 4, :])
+        load_plane(nc.gpsimd, wf_plane, wf_scales)
         wf_raw = tile([P, 2 * H], U8, "wf_raw")
         nc.sync.dma_start(out=wf_raw[:].bitcast(I32), in_=wf_words[0].bitcast(I32))
         tab_w = tile([P, T], I32, "tab_w")
@@ -78,7 +79,10 @@ def tile_list_reaction_rates_kernel(tc, tab_words, tab_scales, tab2_words, tab2_
             in_=ws_words.rearrange("a p n t -> p a (n t)").bitcast(I32),
         )
         ws_plane = tile([P, N], U8, "ws_plane")
-        load_plane(nc.gpsimd, nc.sync, ws_plane, WS_ROW, 8, lambda q: ws_scales[:, 4 * q : 4 * q + 4, :])
+        nc.gpsimd.memset(ws_plane[:].bitcast(I32), 0)
+        for q in range(4):
+            nc.sync.dma_start(out=ws_plane[32 * q + WS_ROW : 32 * q + WS_ROW + 8, :].bitcast(I32),
+                              in_=ws_scales[:, 4 * q : 4 * q + 4, :].bitcast(I32))
 
         kr_t = tile([P, GROUPS, PACK], F32, "kr_t")
         nc.gpsimd.dma_start(out=kr_t[:], in_=kr.rearrange("(g p t) -> p g t", p=P, t=PACK))
@@ -122,24 +126,27 @@ def tile_list_reaction_rates_kernel(tc, tab_words, tab_scales, tab2_words, tab2_
             first = g * PASS + t * P
             exponential(ea[g], t, half, wf_w[:, 2 * first : 2 * (first + P)].bitcast(FP4X4), wf_s[:, first : first + P], v_w, v_s)
 
-        def scale_reverse(g, t, first, width, on_scalar):
-            e = eb[g][:, t, first : first + width]
-            if on_scalar:
-                nc.scalar.activation(e, e, COPY, scale=kr_t[:, g, t : t + 1])
-            else:
-                nc.vector.tensor_scalar(e, e, kr_t[:, g, t : t + 1], None, MULT)
+        backward = {(g, t): eb[g][:, t, :] for g in range(GROUPS) for t in range(PACK)}
 
-        def net_rate(g, first, width):
+        def scale_reverse(g, t, first, width, on_scalar):
             cols = slice(first, first + width)
-            h = tile([P, PACK, width], BF16, "h%d_%d" % (g, first))
-            for t in range(PACK):
-                nc.vector.scalar_tensor_tensor(h[:, t, :], ea[g][:, t, cols], kf_t[:, g, t : t + 1], eb[g][:, t, cols], MULT, SUB)
-            grouped = tile([P, PACK * width], BF16, "h_bf%d_%d" % (g, first))
-            nc.vector.tensor_copy(
-                out=grouped[:].rearrange("p (c i t) -> p c t i", i=4, t=PACK),
-                in_=h[:].rearrange("p t (c i) -> p c t i", i=4),
-            )
-            quantize(grouped[:], h_w[g][:, cols], h_s[g][:, cols])
+            if on_scalar:
+                nc.scalar.activation(backward[g, t][:, cols], eb[g][:, t, cols], COPY, scale=kr_t[:, g, t : t + 1])
+            else:
+                nc.vector.tensor_scalar(backward[g, t][:, cols], eb[g][:, t, cols], kr_t[:, g, t : t + 1], None, MULT)
+
+        def difference(h, g, t, first, width):
+            cols = slice(first, first + width)
+            nc.vector.scalar_tensor_tensor(h[:, t, :], ea[g][:, t, cols], kf_t[:, g, t : t + 1], backward[g, t][:, cols], MULT, SUB)
+
+        def interleave(rows, name, copy):
+            grouped = tile([P, PACK * rows.shape[2]], BF16, name)
+            copy(out=grouped[:].rearrange("p (c i t) -> p c t i", i=4, t=PACK),
+                 in_=rows.rearrange("p t (c i) -> p c t i", i=4))
+            return grouped
+
+        def quantize_h(grouped, g, first, width):
+            quantize(grouped[:], h_w[g][:, first : first + width], h_s[g][:, first : first + width])
 
         y_plane = tile([P, S], U8, "y_plane")
         y_rows = out_0.rearrange("(p t) n -> p t n", t=PACK)
@@ -161,15 +168,28 @@ def tile_list_reaction_rates_kernel(tc, tab_words, tab_scales, tab2_words, tab2_
                             rhs=h_w[g][:, cols].bitcast(FP8X4), rhs_scale=h_s[g][:, cols], start=(g == 0), stop=(g == GROUPS - 1))
                 rows = slice(b * per_bank, (b + 1) * per_bank)
                 nc.scalar.copy(out=y[:, rows, :], in_=acc[:])
+                if rows.stop % 2 == 0:
+                    pair = slice(rows.stop - 2, rows.stop)
+                    nc.sync.dma_start(out=y_rows[:, pair, cols], in_=y[:, pair, :])
+            return y
+
+        def last_production(first, width):
+            cols = slice(first, first + width)
+            y = tile([P, PACK, width], F32, "y%d" % first)
+            accs = [psum.tile([P, width], F32, name="last", tag="first", bufs=4) for t in range(PACK)]
+            for g in range(GROUPS):
+                for t in range(PACK):
+                    nc.tensor.matmul_mx(
+                        out=accs[t][:],
+                        lhsT=ws_w[:, g * N + t * P : g * N + (t + 1) * P].bitcast(FP8X4),
+                        lhsT_scale=ws_s[WS_ROW + 4 * g : P, t * P : (t + 1) * P],
+                        rhs=h_w[g][:, cols].bitcast(FP8X4), rhs_scale=h_s[g][:, cols], start=(g == 0), stop=(g == GROUPS - 1))
+            for t in range(PACK):
+                (nc.vector.tensor_copy if t % 2 else nc.scalar.copy)(out=y[:, t, :], in_=accs[t][:])
             nc.sync.dma_start(out=y_rows[:, :, first : first + width], in_=y[:])
             return y
 
-        def planes(y, first, width, copy):
-            grouped = tile([P, PACK * width], BF16, "y_bf%d" % first)
-            copy(
-                out=grouped[:].rearrange("p (c i t) -> p c t i", i=4, t=PACK),
-                in_=y[:].rearrange("p t (c i) -> p c t i", i=4),
-            )
+        def planes(grouped, first, width):
             codes = tile([P, width], U32, "y_q%d" % first)
             quantize(grouped[:], codes[:], y_plane[:, first : first + width])
             nc.sync.dma_start(out=y_words[:, first : first + width], in_=codes[:].bitcast(I32))
@@ -198,45 +218,62 @@ def tile_list_reaction_rates_kernel(tc, tab_words, tab_scales, tab2_words, tab2_
         )
         v_w[0] = gather(tab_w[:].bitcast(U32), idx, 0, HALF, U32, "v_w")
         v_w[1] = gather(tab_w[:].bitcast(U32), idx, HALF, HALF, U32, "v_w")
+        held = tile([P, S], F32, "held", tag="tab_w")
+        backward[0, 2] = held[:]
         for t in range(PACK):
-            scale_reverse(0, t, 0, S, on_scalar=t >= 2)
-        for t in range(PACK):
-            forward(0, t, 0)
-            forward(0, t, 1)
-        wr_bf1 = tile([P, PACK * PASS], BF16, "wr_bf1", tag="tab_w")
+            scale_reverse(0, t, 0, S, on_scalar=t == 3)
+        for t, half in ((0, 0), (1, 0), (0, 1), (1, 1), (2, 0), (2, 1), (3, 0), (3, 1)):
+            forward(0, t, half)
+        wr_bf1 = tile([P, PACK * PASS], BF16, "wr_bf1")
         for u in range(2):
             cast_wr(wr_raw1, wr_bf1, u)
+        h0 = tile([P, PACK, S], BF16, "h0")
+        for t in range(PACK):
+            difference(h0, 0, t, 0, S)
         quantize(wr_bf1[:], wr_w[1][:], wr_s[1][:])
-        net_rate(0, 0, S)
+        grouped = [interleave(h0[:, :, half * HALF : (half + 1) * HALF], "h0_bf%d" % half, nc.vector.tensor_copy) for half in range(2)]
+        for half in range(2):
+            quantize_h(grouped[half], 0, half * HALF, HALF)
+        for t in range(PACK):
+            forward(1, t, 0)
+        h1 = tile([P, PACK, HALF], BF16, "h1")
         for t in range(PACK):
             reverse(1, t, 0)
             scale_reverse(1, t, 0, HALF, on_scalar=False)
         for t in range(PACK):
-            forward(1, t, 0)
+            difference(h1, 1, t, 0, HALF)
+        ws_s = tile([P, N], U8, "ws_s", tag="wr_bf1")
+        nc.vector.tensor_copy(
+            out=ws_s[:].rearrange("p (t m) -> p t m", t=PACK),
+            in_=ws_plane[:].rearrange("p (m t) -> p t m", t=PACK),
+        )
+        grouped = interleave(h1[:], "h1_bf", nc.vector.tensor_copy)
         ws_w = tile([P, GROUPS * N], U32, "ws_w", tag="wr_raw1")
         nc.vector.tensor_copy(
             out=ws_w[:].rearrange("p (a u t m) -> p a u m t", a=GROUPS, u=2, t=2),
             in_=ws_raw[:].bitcast(U32).rearrange("p (a m u t) -> p a u m t", a=GROUPS, u=2, t=2),
         )
-        ws_s = tile([P, N], U8, "ws_s", tag="tab_w")
-        nc.vector.tensor_copy(
-            out=ws_s[:].rearrange("p (t m) -> p t m", t=PACK),
-            in_=ws_plane[:].rearrange("p (m t) -> p t m", t=PACK),
-        )
-        net_rate(1, 0, HALF)
-        for t in range(PACK):
-            reverse(1, t, 1)
-            scale_reverse(1, t, HALF, HALF, on_scalar=False)
+        quantize_h(grouped, 1, 0, HALF)
         for t in range(PACK):
             forward(1, t, 1)
+        for t in range(PACK):
+            reverse(1, t, 1)
+            scale_reverse(1, t, HALF, HALF, on_scalar=True)
         y0 = production(0, HALF)
-        net_rate(1, HALF, 256)
-        y1 = production(HALF, 256)
-        net_rate(1, HALF + 256, 256)
-        y2 = production(HALF + 256, 256)
-        planes(y0, 0, HALF, nc.scalar.copy)
-        planes(y1, HALF, 256, nc.vector.tensor_copy)
-        planes(y2, HALF + 256, 256, nc.vector.tensor_copy)
-        for q in range(4):
-            (nc.scalar if q % 2 else nc.sync).dma_start(
-                out=out_2[0, 4 * q : 4 * q + 4, :].bitcast(I32), in_=y_plane[32 * q : 32 * q + 4, :].bitcast(I32))
+        h2 = tile([P, PACK, HALF], BF16, "h2")
+        for t in range(PACK):
+            difference(h2, 1, t, HALF, HALF)
+        grouped = [interleave(h2[:, :, k * QUARTER : (k + 1) * QUARTER], "h2_bf%d" % k, nc.vector.tensor_copy) for k in range(2)]
+        quantize_h(grouped[0], 1, HALF, QUARTER)
+        y1 = production(HALF, QUARTER)
+        quantize_h(grouped[1], 1, HALF + QUARTER, QUARTER)
+        y2 = last_production(HALF + QUARTER, QUARTER)
+        y0_bf = interleave(y0[:], "y0_bf", nc.vector.tensor_copy)
+        y1_bf = interleave(y1[:], "y1_bf", nc.vector.tensor_copy)
+        planes(y0_bf, 0, HALF)
+        y2_bf = interleave(y2[:], "y2_bf", nc.vector.tensor_copy)
+        planes(y1_bf, HALF, QUARTER)
+        planes(y2_bf, HALF + QUARTER, QUARTER)
+        for r in range(4):
+            (nc.scalar if r % 2 else nc.sync).dma_start(
+                out=out_2[0, r:16:4, :].bitcast(I32), in_=y_plane[r:P:32, :].bitcast(I32))

from contextlib import ExitStack

import concourse.mybir as mybir

K, H, N, T, T2, S = 512, 1024, 512, 4096, 2048, 1024
FLOPS = 2 * K * H * S * 2 + 2 * H * N * S

F32 = mybir.dt.float32
BF16 = mybir.dt.bfloat16
I32 = mybir.dt.int32
U32 = mybir.dt.uint32
U16 = mybir.dt.uint16
U8 = mybir.dt.uint8
FP8X4 = mybir.dt.float8_e4m3fn_x4
FP4X4 = mybir.dt.float4_e2m1fn_x4
EXP = mybir.ActivationFunctionType.Exp
COPY = mybir.ActivationFunctionType.Copy
MULT = mybir.AluOpType.mult
SUB = mybir.AluOpType.subtract

P = 128
PACK = 4
PASS = P * PACK
GROUPS = H // PASS
HALF = 512
QUARTER = 256
WS_ROW = 8


def tile_list_reaction_rates_kernel(tc, tab_words, tab_scales, tab2_words, tab2_scales, offs, offs2,
                                             wf_words, wf_scales, wr, kf, kr, ws_words, ws_scales,
                                             out_0, out_1, out_2):
    nc = tc.nc
    with ExitStack() as ctx:
        lists = ctx.enter_context(tc.tile_pool(name="lists", bufs=1))
        keep = ctx.enter_context(tc.tile_pool(name="keep", bufs=1))
        psum = ctx.enter_context(tc.psum_pool(name="psum", bufs=1))

        def tile(shape, dtype, name, tag=None):
            return keep.tile(shape, dtype, name=name, tag=tag or name, align_bytes=64)

        def load_plane(memset_engine, plane, scales):
            memset_engine.memset(plane[:].bitcast(I32), 0)
            for r in range(4):
                nc.sync.dma_start(out=plane[r:P:32, :].bitcast(I32), in_=scales[0, r:16:4, :].bitcast(I32))

        warm = tile([P, 2], F32, "warm")
        nc.vector.memset(warm[:, 0:1], 0.0)
        nc.scalar.activation(warm[:, 1:2], warm[:, 0:1], EXP)
        idx2 = lists.tile([P, S // 16], U16, name="idx2")
        nc.sync.dma_start(idx2[:], offs2)
        tab2_plane = tile([P, T2], U8, "tab2_plane")
        for q in range(4):
            nc.sync.dma_start(out=tab2_plane[32 * q : 32 * q + 32, :].bitcast(I32),
                              in_=tab2_scales[0, 4 * q : 4 * q + 4, :].bitcast(I32).unsqueeze(0).broadcast_to([8, 4, T2 // 4]))
        idx = lists.tile([P, S // 16], U16, name="idx")
        nc.sync.dma_start(idx[:], offs)
        tab2_w = tile([P, T2], I32, "tab2_w")
        nc.sync.dma_start(out=tab2_w[:], in_=tab2_words[0].rearrange("p n t -> p (n t)").bitcast(I32))
        tab_plane = tile([P, T], U8, "tab_plane")
        load_plane(nc.vector, tab_plane, tab_scales)

        def load_wr(g):
            raw = tile([P, PACK, PASS], F32, "wr_raw%d" % g)
            nc.sync.dma_start(out=raw[:], in_=wr[:, g * PASS : (g + 1) * PASS].rearrange("(p j) c -> p j c", j=PACK))
            return raw

        wr_raw0 = load_wr(0)
        wf_plane = tile([P, H], U8, "wf_plane")
        load_plane(nc.gpsimd, wf_plane, wf_scales)
        wf_raw = tile([P, 2 * H], U8, "wf_raw")
        nc.sync.dma_start(out=wf_raw[:].bitcast(I32), in_=wf_words[0].bitcast(I32))
        tab_w = tile([P, T], I32, "tab_w")
        nc.sync.dma_start(out=tab_w[:], in_=tab_words[0].rearrange("p n t -> p (n t)").bitcast(I32))
        wr_raw1 = load_wr(1)
        ws_raw = tile([P, GROUPS * N], I32, "ws_raw")
        nc.sync.dma_start(
            out=ws_raw[:].rearrange("p (a n) -> p a n", a=GROUPS),
            in_=ws_words.rearrange("a p n t -> p a (n t)").bitcast(I32),
        )
        ws_plane = tile([P, N], U8, "ws_plane")
        nc.gpsimd.memset(ws_plane[:].bitcast(I32), 0)
        for q in range(4):
            nc.sync.dma_start(out=ws_plane[32 * q + WS_ROW : 32 * q + WS_ROW + 8, :].bitcast(I32),
                              in_=ws_scales[:, 4 * q : 4 * q + 4, :].bitcast(I32))

        kr_t = tile([P, GROUPS, PACK], F32, "kr_t")
        nc.gpsimd.dma_start(out=kr_t[:], in_=kr.rearrange("(g p t) -> p g t", p=P, t=PACK))
        kf_t = tile([P, GROUPS, PACK], F32, "kf_t")
        nc.gpsimd.dma_start(out=kf_t[:], in_=kf.rearrange("(g p t) -> p g t", p=P, t=PACK))

        def gather(window, offsets, first, count, dtype, name):
            got = tile([P, count], dtype, "%s%d" % (name, first))
            nc.vector.tensor_copy(got[:], window.indirect(offsets[:, first // 16 : (first + count) // 16]))
            return got

        def quantize(grouped, codes, plane):
            nc.vector.quantize_mx(out=codes.bitcast(FP8X4), scales=plane, in_=grouped)

        def cast_wr(raw, grouped, u):
            nc.scalar.copy(
                out=grouped[:, 2 * u * PASS : 2 * (u + 1) * PASS].rearrange("p (t m j) -> p m j t", t=2, j=PACK),
                in_=raw[:].rearrange("p j (m u t) -> p u m j t", u=2, t=2)[:, u],
            )

        wr_w = [tile([P, PASS], U32, "wr_w%d" % g) for g in range(GROUPS)]
        wr_s = [tile([P, PASS], U8, "wr_s%d" % g) for g in range(GROUPS)]
        ea = [tile([P, PACK, S], F32, "ea%d" % g) for g in range(GROUPS)]
        eb = [tile([P, PACK, S], F32, "eb%d" % g) for g in range(GROUPS)]
        h_w = [tile([P, S], U32, "h_w%d" % g) for g in range(GROUPS)]
        h_s = [tile([P, S], U8, "h_s%d" % g) for g in range(GROUPS)]
        v_w, v2_w = {}, {}

        def exponential(e, t, half, w, w_scale, cells, cells_scale):
            acc = psum.tile([P, HALF], F32, name="first", tag="first", bufs=4)
            cols = slice(half * HALF, (half + 1) * HALF)
            nc.tensor.matmul_mx(out=acc[:], lhsT=w, lhsT_scale=w_scale, rhs=cells[half][:].bitcast(FP8X4),
                                rhs_scale=cells_scale[:, cols], start=True, stop=True)
            nc.scalar.activation(e[:, t, cols], acc[:], EXP)

        def reverse(g, t, half):
            cols = slice(t * P, (t + 1) * P)
            exponential(eb[g], t, half, wr_w[g][:, cols].bitcast(FP8X4), wr_s[g][:, cols], v2_w, v2_s)

        def forward(g, t, half):
            first = g * PASS + t * P
            exponential(ea[g], t, half, wf_w[:, 2 * first : 2 * (first + P)].bitcast(FP4X4), wf_s[:, first : first + P], v_w, v_s)

        backward = {(g, t): eb[g][:, t, :] for g in range(GROUPS) for t in range(PACK)}

        def scale_reverse(g, t, first, width, on_scalar):
            cols = slice(first, first + width)
            if on_scalar:
                nc.scalar.activation(backward[g, t][:, cols], eb[g][:, t, cols], COPY, scale=kr_t[:, g, t : t + 1])
            else:
                nc.vector.tensor_scalar(backward[g, t][:, cols], eb[g][:, t, cols], kr_t[:, g, t : t + 1], None, MULT)

        def difference(h, g, t, first, width):
            cols = slice(first, first + width)
            nc.vector.scalar_tensor_tensor(h[:, t, :], ea[g][:, t, cols], kf_t[:, g, t : t + 1], backward[g, t][:, cols], MULT, SUB)

        def interleave(rows, name, copy):
            grouped = tile([P, PACK * rows.shape[2]], BF16, name)
            copy(out=grouped[:].rearrange("p (c i t) -> p c t i", i=4, t=PACK),
                 in_=rows.rearrange("p t (c i) -> p c t i", i=4))
            return grouped

        def quantize_h(grouped, g, first, width):
            quantize(grouped[:], h_w[g][:, first : first + width], h_s[g][:, first : first + width])

        y_plane = tile([P, S], U8, "y_plane")
        y_rows = out_0.rearrange("(p t) n -> p t n", t=PACK)
        y_words = out_1[0].rearrange("p n t -> p (n t)").bitcast(I32)

        def production(first, width):
            cols = slice(first, first + width)
            y = tile([P, PACK, width], F32, "y%d" % first)
            per_bank = HALF // width
            for b in range(PACK // per_bank):
                acc = psum.tile([P, per_bank, width], F32, name="second", tag="second", bufs=4)
                for s in range(per_bank):
                    t = b * per_bank + s
                    for g in range(GROUPS):
                        nc.tensor.matmul_mx(
                            out=acc[:, s, :],
                            lhsT=ws_w[:, g * N + t * P : g * N + (t + 1) * P].bitcast(FP8X4),
                            lhsT_scale=ws_s[WS_ROW + 4 * g : P, t * P : (t + 1) * P],
                            rhs=h_w[g][:, cols].bitcast(FP8X4), rhs_scale=h_s[g][:, cols], start=(g == 0), stop=(g == GROUPS - 1))
                rows = slice(b * per_bank, (b + 1) * per_bank)
                nc.scalar.copy(out=y[:, rows, :], in_=acc[:])
                if rows.stop % 2 == 0:
                    pair = slice(rows.stop - 2, rows.stop)
                    nc.sync.dma_start(out=y_rows[:, pair, cols], in_=y[:, pair, :])
            return y

        def last_production(first, width):
            cols = slice(first, first + width)
            y = tile([P, PACK, width], F32, "y%d" % first)
            accs = [psum.tile([P, width], F32, name="last", tag="first", bufs=4) for t in range(PACK)]
            for g in range(GROUPS):
                for t in range(PACK):
                    nc.tensor.matmul_mx(
                        out=accs[t][:],
                        lhsT=ws_w[:, g * N + t * P : g * N + (t + 1) * P].bitcast(FP8X4),
                        lhsT_scale=ws_s[WS_ROW + 4 * g : P, t * P : (t + 1) * P],
                        rhs=h_w[g][:, cols].bitcast(FP8X4), rhs_scale=h_s[g][:, cols], start=(g == 0), stop=(g == GROUPS - 1))
            for t in range(PACK):
                (nc.vector.tensor_copy if t % 2 else nc.scalar.copy)(out=y[:, t, :], in_=accs[t][:])
            nc.sync.dma_start(out=y_rows[:, :, first : first + width], in_=y[:])
            return y

        def planes(grouped, first, width):
            codes = tile([P, width], U32, "y_q%d" % first)
            quantize(grouped[:], codes[:], y_plane[:, first : first + width])
            nc.sync.dma_start(out=y_words[:, first : first + width], in_=codes[:].bitcast(I32))

        v2_s = gather(tab2_plane[:], idx2, 0, S, U8, "v2_s")
        v2_w[0] = gather(tab2_w[:].bitcast(U32), idx2, 0, HALF, U32, "v2_w")
        v2_w[1] = gather(tab2_w[:].bitcast(U32), idx2, HALF, HALF, U32, "v2_w")
        wr_bf0 = tile([P, PACK * PASS], BF16, "wr_bf0")
        for u in range(2):
            cast_wr(wr_raw0, wr_bf0, u)
            cols = slice(2 * u * P, 2 * (u + 1) * P)
            quantize(wr_bf0[:, 2 * u * PASS : 2 * (u + 1) * PASS], wr_w[0][:, cols], wr_s[0][:, cols])
        v_s = gather(tab_plane[:], idx, 0, S, U8, "v_s")
        for t in range(PACK):
            reverse(0, t, 0)
            reverse(0, t, 1)
        wf_w = tile([P, 2 * H], U8, "wf_w")
        nc.vector.tensor_copy(
            out=wf_w[:].bitcast(U16).rearrange("p (g t m) -> p g t m", g=GROUPS, t=PACK),
            in_=wf_raw[:].bitcast(U16).rearrange("p (g m t) -> p g t m", g=GROUPS, t=PACK),
        )
        wf_s = tile([P, H], U8, "wf_s")
        nc.vector.tensor_copy(
            out=wf_s[:].rearrange("p (g t m) -> p g t m", g=GROUPS, t=PACK),
            in_=wf_plane[:].rearrange("p (g m t) -> p g t m", g=GROUPS, t=PACK),
        )
        v_w[0] = gather(tab_w[:].bitcast(U32), idx, 0, HALF, U32, "v_w")
        v_w[1] = gather(tab_w[:].bitcast(U32), idx, HALF, HALF, U32, "v_w")
        held = tile([P, S], F32, "held", tag="tab_w")
        backward[0, 2] = held[:]
        for t in range(PACK):
            scale_reverse(0, t, 0, S, on_scalar=t == 3)
        for t, half in ((0, 0), (1, 0), (0, 1), (1, 1), (2, 0), (2, 1), (3, 0), (3, 1)):
            forward(0, t, half)
        wr_bf1 = tile([P, PACK * PASS], BF16, "wr_bf1")
        for u in range(2):
            cast_wr(wr_raw1, wr_bf1, u)
        h0 = tile([P, PACK, S], BF16, "h0")
        for t in range(PACK):
            difference(h0, 0, t, 0, S)
        quantize(wr_bf1[:], wr_w[1][:], wr_s[1][:])
        grouped = [interleave(h0[:, :, half * HALF : (half + 1) * HALF], "h0_bf%d" % half, nc.vector.tensor_copy) for half in range(2)]
        for half in range(2):
            quantize_h(grouped[half], 0, half * HALF, HALF)
        for t in range(PACK):
            forward(1, t, 0)
        h1 = tile([P, PACK, HALF], BF16, "h1")
        for t in range(PACK):
            reverse(1, t, 0)
            scale_reverse(1, t, 0, HALF, on_scalar=False)
        for t in range(PACK):
            difference(h1, 1, t, 0, HALF)
        ws_s = tile([P, N], U8, "ws_s", tag="wr_bf1")
        nc.vector.tensor_copy(
            out=ws_s[:].rearrange("p (t m) -> p t m", t=PACK),
            in_=ws_plane[:].rearrange("p (m t) -> p t m", t=PACK),
        )
        grouped = interleave(h1[:], "h1_bf", nc.vector.tensor_copy)
        ws_w = tile([P, GROUPS * N], U32, "ws_w", tag="wr_raw1")
        nc.vector.tensor_copy(
            out=ws_w[:].rearrange("p (a u t m) -> p a u m t", a=GROUPS, u=2, t=2),
            in_=ws_raw[:].bitcast(U32).rearrange("p (a m u t) -> p a u m t", a=GROUPS, u=2, t=2),
        )
        quantize_h(grouped, 1, 0, HALF)
        for t in range(PACK):
            forward(1, t, 1)
        for t in range(PACK):
            reverse(1, t, 1)
            scale_reverse(1, t, HALF, HALF, on_scalar=True)
        y0 = production(0, HALF)
        h2 = tile([P, PACK, HALF], BF16, "h2")
        for t in range(PACK):
            difference(h2, 1, t, HALF, HALF)
        grouped = [interleave(h2[:, :, k * QUARTER : (k + 1) * QUARTER], "h2_bf%d" % k, nc.vector.tensor_copy) for k in range(2)]
        quantize_h(grouped[0], 1, HALF, QUARTER)
        y1 = production(HALF, QUARTER)
        quantize_h(grouped[1], 1, HALF + QUARTER, QUARTER)
        y2 = last_production(HALF + QUARTER, QUARTER)
        y0_bf = interleave(y0[:], "y0_bf", nc.vector.tensor_copy)
        y1_bf = interleave(y1[:], "y1_bf", nc.vector.tensor_copy)
        planes(y0_bf, 0, HALF)
        y2_bf = interleave(y2[:], "y2_bf", nc.vector.tensor_copy)
        planes(y1_bf, HALF, QUARTER)
        planes(y2_bf, HALF + QUARTER, QUARTER)
        for r in range(4):
            (nc.scalar if r % 2 else nc.sync).dma_start(
                out=out_2[0, r:16:4, :].bitcast(I32), in_=y_plane[r:P:32, :].bitcast(I32))
